import numpy as np
import ml_dtypes


def mxq(x, axis, fmt="e4m3"):
    dtype, down = {"e4m3": (ml_dtypes.float8_e4m3fn, 7), "e5m2": (ml_dtypes.float8_e5m2, 14)}[fmt]
    v = np.moveaxis(np.asarray(x, np.float32).astype(ml_dtypes.bfloat16).astype(np.float64), axis, -1)
    blocks = v.reshape(v.shape[:-1] + (-1, 32))
    amax = np.abs(blocks).max(-1, keepdims=True)
    byte = np.maximum(np.where(amax > 0, np.frexp(amax)[1] - 1 + 127, 0) - down, 1)
    scale = np.exp2(byte - 127.0)
    codes = (blocks / scale).astype(np.float32).astype(dtype).astype(np.float64)
    return np.moveaxis((codes * scale).reshape(v.shape), -1, axis)


WIDE = False


def mx_kscale(k):
    if not WIDE:
        return np.ones(k)
    levels = np.array([10, -10, 5, -5, 0])
    if k % 512:
        return np.exp2(np.random.permutation(np.resize(levels, k // 32))).repeat(32)
    a = np.empty((k // 512, 16))
    for p in range(k // 512):
        a[p, :8] = np.random.permutation(np.resize(levels, 8))
        for g in range(8):
            far = levels[np.abs(levels - a[p, g]) >= 10]
            a[p, g + 8] = far[np.random.randint(len(far))]
    return np.exp2(a.ravel()).repeat(32)


BF16 = ml_dtypes.bfloat16


def bf(x):
    return np.asarray(x, np.float32).astype(BF16)


def f64(x):
    return np.asarray(x).astype(np.float64)

def planes(Y):
    n, m = Y.shape
    b = f64(bf(Y)).reshape(n // 32, 32, m)
    amax = np.abs(b).max(1)
    byte = np.clip(np.where(amax > 0, np.frexp(amax)[1] - 1 + 127 - 7, 1), 1, 254)
    codes = (b * np.exp2(127.0 - byte)[:, None, :]).reshape(n, m).astype(np.float32).astype(ml_dtypes.float8_e4m3fn).view(np.uint8)
    words = codes.reshape(n // 512, 128, 4, m).transpose(0, 1, 3, 2)
    return np.ascontiguousarray(words), np.ascontiguousarray(byte.astype(np.uint8).reshape(n // 512, 16, m))


T, J, M, N = 2048, 1536, 1024, 512

def setup_inputs():
    s = mx_kscale(J)
    t = mx_kscale(T)
    plan = np.random.randn(T, J) * s[None, :] * t[:, None]
    hours = np.exp(1.2 * np.random.randn(J, M) - 1.44) / np.sqrt(J) / s[:, None]
    spare = np.abs(0.5 * np.random.randn(T, M)) * t[:, None]
    rates = 2.0 * np.random.randn(N, T) / np.sqrt(T) / t[None, :]
    budgets = np.exp(0.8 * np.random.randn(N))
    return {"plan": bf(plan), "hours": bf(hours), "spare": bf(spare),
            "rates": bf(rates), "budgets": bf(budgets)}

def reference(plan, hours, spare, rates, budgets):
    plan, hours, spare = f64(plan), f64(hours), f64(spare)
    rates, budgets = f64(rates), f64(budgets)
    load = mxq(plan, 1, "e4m3") @ mxq(hours, 0, "e4m3")
    over = np.maximum(load - spare, 0.0)
    cost = mxq(rates, 1, "e4m3") @ mxq(over, 0, "e4m3")
    y = cost * budgets[:, None]
    Y = y.reshape(N, M)
    words, scales = planes(Y)
    return y, words, scales

from contextlib import ExitStack

import concourse.mybir as mybir
from concourse.masks import make_identity

T, J, M, N = 2048, 1536, 1024, 512
FLOPS = 2 * T * J * M + 2 * N * T * M

F32 = mybir.dt.float32
BF16 = mybir.dt.bfloat16
U32 = mybir.dt.uint32
I32 = mybir.dt.int32
U8 = mybir.dt.uint8
FP8X4 = mybir.dt.float8_e4m3fn_x4
ALU = mybir.AluOpType
ACT = mybir.ActivationFunctionType

P = 128
K_PASS = 512
GROUPS = T // K_PASS
J_PASSES = J // K_PASS
QUARTERS = 4
W = M // QUARTERS

def program():
    return [('turn', ('plan', 0, 0, 0)),
        ('leave', ('plan', 0, 0, 0)),
        ('turn', ('plan', 0, 0, 1)),
        ('leave', ('plan', 0, 0, 1)),
        ('turn', ('plan', 0, 0, 2)),
        ('pack', ('plan', 0, 0, 0)),
        ('weave', ('hours', 0, 0), 'vector'),
        ('leave', ('plan', 0, 0, 2)),
        ('pack', ('plan', 0, 0, 1)),
        ('pack', ('plan', 0, 0, 2)),
        ('weave', ('hours', 2, 0), 'scalar'),
        ('pack', ('hours', 0, 0)),
        ('weave', ('hours', 1, 0), 'vector'),
        ('pack', ('hours', 2, 0)),
        ('pack', ('hours', 1, 0)),
        ('turn', ('plan', 0, 1, 0)),
        ('leave', ('plan', 0, 1, 0)),
        ('turn', ('plan', 0, 1, 1)),
        ('leave', ('plan', 0, 1, 1)),
        ('turn', ('plan', 0, 1, 2)),
        ('pack', ('plan', 0, 1, 0)),
        ('leave', ('plan', 0, 1, 2)),
        ('pack', ('plan', 0, 1, 1)),
        ('load', 0, 0, 0),
        ('pack', ('plan', 0, 1, 2)),
        ('turn', ('plan', 1, 0, 0)),
        ('sub', 0, 0, 0),
        ('leave', ('plan', 1, 0, 0)),
        ('turn', ('plan', 1, 0, 1)),
        ('leave', ('plan', 1, 0, 1)),
        ('turn', ('plan', 1, 0, 2)),
        ('pack', ('plan', 1, 0, 0)),
        ('leave', ('plan', 1, 0, 2)),
        ('pack', ('plan', 1, 0, 1)),
        ('load', 0, 0, 1),
        ('weave', ('hours', 0, 1), 'scalar'),
        ('pack', ('plan', 1, 0, 2)),
        ('turn', ('plan', 1, 1, 0)),
        ('sub', 0, 0, 1),
        ('turn', ('plan', 1, 1, 1)),
        ('weave', ('hours', 1, 1), 'scalar'),
        ('clamp', 0, 0),
        ('turn', ('plan', 1, 1, 2)),
        ('pack', ('hours', 0, 1)),
        ('pack', ('over', 0, 0)),
        ('load', 1, 0, 0),
        ('leave', ('plan', 1, 1, 0)),
        ('pack', ('hours', 1, 1)),
        ('sub', 1, 0, 0),
        ('leave', ('plan', 1, 1, 1)),
        ('turn', ('plan', 2, 0, 0)),
        ('pack', ('plan', 1, 1, 0)),
        ('leave', ('plan', 1, 1, 2)),
        ('turn', ('plan', 2, 0, 1)),
        ('pack', ('plan', 1, 1, 1)),
        ('leave', ('plan', 2, 0, 0)),
        ('turn', ('plan', 2, 0, 2)),
        ('pack', ('plan', 1, 1, 2)),
        ('leave', ('plan', 2, 0, 1)),
        ('pack', ('plan', 2, 0, 0)),
        ('leave', ('plan', 2, 0, 2)),
        ('load', 1, 0, 1),
        ('pack', ('plan', 2, 0, 1)),
        ('sub', 1, 0, 1),
        ('weave', ('hours', 2, 1), 'scalar'),
        ('turn', ('plan', 2, 1, 0)),
        ('pack', ('plan', 2, 0, 2)),
        ('turn', ('plan', 2, 1, 1)),
        ('clamp', 1, 0),
        ('turn', ('plan', 2, 1, 2)),
        ('leave', ('plan', 2, 1, 0)),
        ('pack', ('over', 1, 0)),
        ('pack', ('hours', 2, 1)),
        ('leave', ('plan', 2, 1, 1)),
        ('pack', ('plan', 2, 1, 0)),
        ('load', 2, 0, 0),
        ('leave', ('plan', 2, 1, 2)),
        ('pack', ('plan', 2, 1, 1)),
        ('turn', ('plan', 3, 0, 0)),
        ('sub', 2, 0, 0),
        ('leave', ('plan', 3, 0, 0)),
        ('turn', ('plan', 3, 0, 1)),
        ('pack', ('plan', 2, 1, 2)),
        ('leave', ('plan', 3, 0, 1)),
        ('turn', ('plan', 3, 0, 2)),
        ('pack', ('plan', 3, 0, 0)),
        ('leave', ('plan', 3, 0, 2)),
        ('pack', ('plan', 3, 0, 1)),
        ('load', 2, 0, 1),
        ('pack', ('plan', 3, 0, 2)),
        ('turn', ('plan', 3, 1, 0)),
        ('sub', 2, 0, 1),
        ('leave', ('plan', 3, 1, 0)),
        ('turn', ('plan', 3, 1, 1)),
        ('clamp', 2, 0),
        ('leave', ('plan', 3, 1, 1)),
        ('turn', ('plan', 3, 1, 2)),
        ('pack', ('plan', 3, 1, 0)),
        ('pack', ('over', 2, 0)),
        ('leave', ('plan', 3, 1, 2)),
        ('pack', ('plan', 3, 1, 1)),
        ('load', 3, 0, 0),
        ('weave', ('hours', 0, 2), 'scalar'),
        ('pack', ('plan', 3, 1, 2)),
        ('sub', 3, 0, 0),
        ('load', 3, 0, 1),
        ('weave', ('hours', 1, 2), 'scalar'),
        ('pack', ('hours', 0, 2)),
        ('sub', 3, 0, 1),
        ('load', 0, 1, 0),
        ('sub', 0, 1, 0),
        ('weave', ('hours', 2, 2), 'scalar'),
        ('load', 0, 1, 1),
        ('clamp', 3, 0),
        ('sub', 0, 1, 1),
        ('turn', ('rates', 0, 0)),
        ('pack', ('over', 3, 0)),
        ('leave', ('rates', 0, 0)),
        ('turn', ('rates', 0, 1)),
        ('clamp', 0, 1),
        ('leave', ('rates', 0, 1)),
        ('pack', ('hours', 1, 2)),
        ('pack', ('over', 0, 1)),
        ('load', 1, 1, 0),
        ('pack', ('rates', 0, 0)),
        ('pack', ('rates', 0, 1)),
        ('sub', 1, 1, 0),
        ('load', 1, 1, 1),
        ('weave', ('hours', 0, 3), 'scalar'),
        ('pack', ('hours', 2, 2)),
        ('turn', ('rates', 1, 0)),
        ('sub', 1, 1, 1),
        ('turn', ('rates', 1, 1)),
        ('clamp', 1, 1),
        ('weave', ('hours', 1, 3), 'scalar'),
        ('pack', ('hours', 0, 3)),
        ('load', 2, 1, 0),
        ('pack', ('over', 1, 1)),
        ('sub', 2, 1, 0),
        ('load', 2, 1, 1),
        ('leave', ('rates', 1, 0)),
        ('pack', ('hours', 1, 3)),
        ('sub', 2, 1, 1),
        ('turn', ('rates', 2, 0)),
        ('leave', ('rates', 1, 1)),
        ('turn', ('rates', 2, 1)),
        ('pack', ('rates', 1, 0)),
        ('weave', ('hours', 2, 3), 'scalar'),
        ('pack', ('rates', 1, 1)),
        ('clamp', 2, 1),
        ('load', 3, 1, 0),
        ('pack', ('over', 2, 1)),
        ('leave', ('rates', 2, 0)),
        ('sub', 3, 1, 0),
        ('load', 3, 1, 1),
        ('leave', ('rates', 2, 1)),
        ('pack', ('rates', 2, 0)),
        ('sub', 3, 1, 1),
        ('turn', ('rates', 3, 0)),
        ('leave', ('rates', 3, 0)),
        ('turn', ('rates', 3, 1)),
        ('pack', ('rates', 2, 1)),
        ('clamp', 3, 1),
        ('leave', ('rates', 3, 1)),
        ('pack', ('rates', 3, 0)),
        ('load', 0, 2, 0),
        ('pack', ('over', 3, 1)),
        ('pack', ('rates', 3, 1)),
        ('sub', 0, 2, 0),
        ('load', 0, 2, 1),
        ('pack', ('hours', 2, 3)),
        ('sub', 0, 2, 1),
        ('cost', 0, 0),
        ('clamp', 0, 2),
        ('scale', 0, 0),
        ('cost', 0, 1),
        ('pack', ('over', 0, 2)),
        ('scale', 0, 1),
        ('load', 1, 2, 0),
        ('store_y', 0),
        ('sub', 1, 2, 0),
        ('load', 1, 2, 1),
        ('round', 0),
        ('load', 2, 2, 0),
        ('sub', 1, 2, 1),
        ('pack', ('y', 0)),
        ('load', 2, 2, 1),
        ('clamp', 1, 2),
        ('store_words', 0),
        ('sub', 2, 2, 0),
        ('pack', ('over', 1, 2)),
        ('cost', 1, 0),
        ('sub', 2, 2, 1),
        ('scale', 1, 0),
        ('clamp', 2, 2),
        ('cost', 1, 1),
        ('pack', ('over', 2, 2)),
        ('scale', 1, 1),
        ('load', 3, 2, 0),
        ('store_y', 1),
        ('sub', 3, 2, 0),
        ('load', 3, 2, 1),
        ('round', 1),
        ('load', 0, 3, 0),
        ('sub', 3, 2, 1),
        ('pack', ('y', 1)),
        ('load', 0, 3, 1),
        ('clamp', 3, 2),
        ('store_words', 1),
        ('sub', 0, 3, 0),
        ('load', 1, 3, 0),
        ('pack', ('over', 3, 2)),
        ('sub', 0, 3, 1),
        ('load', 1, 3, 1),
        ('sub', 1, 3, 0),
        ('clamp', 0, 3),
        ('load', 2, 3, 0),
        ('sub', 1, 3, 1),
        ('load', 2, 3, 1),
        ('pack', ('over', 0, 3)),
        ('clamp', 1, 3),
        ('sub', 2, 3, 0),
        ('load', 3, 3, 0),
        ('pack', ('over', 1, 3)),
        ('sub', 2, 3, 1),
        ('load', 3, 3, 1),
        ('sub', 3, 3, 0),
        ('clamp', 2, 3),
        ('cost', 2, 0),
        ('sub', 3, 3, 1),
        ('pack', ('over', 2, 3)),
        ('scale', 2, 0),
        ('clamp', 3, 3),
        ('cost', 2, 1),
        ('pack', ('over', 3, 3)),
        ('scale', 2, 1),
        ('store_y', 2),
        ('round', 2),
        ('cost', 3, 0),
        ('pack', ('y', 2)),
        ('scale', 3, 0),
        ('cost', 3, 1),
        ('store_words', 2),
        ('store_scales', 0, 3),
        ('scale', 3, 1),
        ('store_y', 3),
        ('round', 3),
        ('pack', ('y', 3)),
        ('store_words', 3),
        ('store_scales', 3, 4)]


def tile_plant_overtime_cost_h3_kernel(tc, plan, hours, spare, rates, budgets, out_0, out_1, out_2):
    nc = tc.nc
    with ExitStack() as ctx:
        keep = ctx.enter_context(tc.tile_pool(name="keep", bufs=1))
        work = ctx.enter_context(tc.tile_pool(name="work", bufs=3))
        psum = ctx.enter_context(tc.psum_pool(name="psum", bufs=8))
        ctx.enter_context(tc.manual_schedule())

        def mx_pair(name, width):
            codes = keep.tile([P, width], U32, name=name + "_codes", align_bytes=64)
            scales = keep.tile([P, width], U8, name=name + "_scales", align_bytes=64)
            return codes, scales

        plan_mx = {(g, c): mx_pair("plan%d%d" % (g, c), 4 * P) for g in range(GROUPS) for c in range(J_PASSES)}
        hours_mx = [mx_pair("hours%d" % c, M) for c in range(J_PASSES)]
        rates_mx = [mx_pair("rates%d" % t, GROUPS * P) for t in range(4)]
        over_mx = [mx_pair("over%d" % g, M) for g in range(GROUPS)]
        y_mx = mx_pair("y", M)

        def quantise(mx, cols, src):
            nc.vector.quantize_mx(out=mx[0][:, cols].bitcast(FP8X4), scales=mx[1][:, cols], in_=src)

        def matmul(out, lhs, lhs_cols, rhs, rhs_cols, start, stop):
            nc.tensor.matmul_mx(
                out=out,
                lhsT=lhs[0][:, lhs_cols].bitcast(FP8X4),
                lhsT_scale=lhs[1][:, lhs_cols],
                rhs=rhs[0][:, rhs_cols].bitcast(FP8X4),
                rhs_scale=rhs[1][:, rhs_cols],
                start=start,
                stop=stop,
            )

        def quarter(q):
            return slice(q * W, (q + 1) * W)

        ident = keep.tile([P, P], F32, name="ident")
        make_identity(nc, ident[:])
        budget_bf = keep.tile([P, 4], BF16, name="budget_bf")
        budget = keep.tile([P, 4], F32, name="budget")
        nc.scalar.dma_start(out=budget_bf[:], in_=budgets.rearrange("(p t) -> p t", t=4))
        nc.scalar.activation(out=budget[:], in_=budget_bf[:], func=ACT.Copy)

        plan_rows, rates_rows, hours_rows, spare_rows = {}, {}, {}, {}

        def load_plan(g, h, pieces=1):
            rows = work.tile([P, 2, J], BF16, name="rows", bufs=5)
            src = plan[g * K_PASS : (g + 1) * K_PASS, :].rearrange("(p t) k -> p t k", t=4)
            nc.sync.dma_start(out=rows[:], in_=src[:, 2 * h : 2 * h + 2, :])
            for c in range(J_PASSES):
                plan_rows[g, h, c] = rows[:, :, c * K_PASS : (c + 1) * K_PASS]

        def load_plan_pass(g, h, c):
            rows = keep.tile([P, 2, K_PASS], BF16, name="first_rows%d" % c)
            src = plan[g * K_PASS : (g + 1) * K_PASS, :].rearrange("(p t) k -> p t k", t=4)
            nc.sync.dma_start(out=rows[:], in_=src[:, 2 * h : 2 * h + 2, c * K_PASS : (c + 1) * K_PASS])
            plan_rows[g, h, c] = rows[:]

        def load_rates(t):
            rows = work.tile([P, GROUPS, K_PASS], BF16, name="rows", bufs=5)
            src = rates.rearrange("(p t) (g k) -> p t g k", t=4, k=K_PASS)
            nc.sync.dma_start(out=rows[:], in_=src[:, t, :, :])
            rates_rows[t] = rows

        def load_hours(q):
            for c in range(J_PASSES):
                rows = keep.tile([P, 4, W], BF16, name="hours_rows%d%d" % (c, q))
                src = hours[c * K_PASS : (c + 1) * K_PASS, :].rearrange("(p t) m -> p t m", t=4)
                nc.sync.dma_start(out=rows[:], in_=src[:, :, quarter(q)])
                hours_rows[c, q] = rows

        def load_spare(g, q0, nq):
            rows = keep.tile([P, 4, nq * W], BF16, name="spare_rows%d%d" % (g, q0))
            src = spare[g * K_PASS : (g + 1) * K_PASS, :].rearrange("(p t) m -> p t m", t=4)
            nc.sync.dma_start(out=rows[:], in_=src[:, :, q0 * W : (q0 + nq) * W])
            for i in range(nq):
                spare_rows[g, q0 + i] = rows[:, :, quarter(i)]

        for c in range(J_PASSES):
            load_plan_pass(0, 0, c)
        load_hours(0)
        load_plan(0, 1)
        load_spare(0, 0, 1)
        load_plan(1, 0)
        load_plan(1, 1)
        load_spare(1, 0, 1)
        load_hours(1)
        for g in (2, 3):
            load_plan(g, 0)
            load_spare(g, 0, 1)
            load_plan(g, 1)
        load_spare(0, 1, 1)
        load_rates(0)
        load_spare(1, 1, 1)
        load_rates(1)
        load_hours(2)
        load_spare(2, 1, 1)
        load_rates(2)
        load_spare(3, 1, 1)
        load_rates(3)
        load_spare(0, 2, 2)
        load_hours(3)
        for g in (1, 2, 3):
            load_spare(g, 2, 2)

        banks, staged, pairs, y_tiles = {}, {}, {}, {}

        def turn(key):
            src = plan_rows[key[1:]] if key[0] == "plan" else rates_rows[key[1]][:, 2 * key[2] : 2 * key[2] + 2, :]
            bank = psum.tile([P, 2, 2, P], F32, name="bank")
            words = src.bitcast(F32)
            for e in range(2):
                for w in range(2):
                    nc.tensor.transpose(bank[:, e, w, :], words[:, e, w : 2 * P : 2], ident[:])
            banks[key] = bank

        def leave(key):
            grouped = work.tile([P, 2 * P * 4], BF16, name="grouped", bufs=4, align_bytes=64)
            nc.scalar.copy(
                out=grouped[:].bitcast(F32).rearrange("p (e r w) -> p e r w", e=2, w=2),
                in_=banks[key][:].rearrange("p e w r -> p e r w"),
            )
            staged[key] = grouped

        def weave(key, engine):
            grouped = work.tile([P, W * 4], BF16, name="hours_grouped", bufs=3, align_bytes=64)
            src = hours_rows[key[1:]][:].rearrange("p t m -> p m t")
            dst = grouped[:].rearrange("p (m t) -> p m t", t=4)
            if engine == "vector":
                nc.vector.tensor_copy(out=dst, in_=src)
            else:
                nc.scalar.copy(out=dst, in_=src)
            staged[key] = grouped

        def pack(key):
            if key[0] == "plan":
                mx, cols = plan_mx[key[1], key[3]], quarter(key[2])
            elif key[0] == "rates":
                mx, cols = rates_mx[key[1]], quarter(key[2])
            elif key[0] == "hours":
                mx, cols = hours_mx[key[1]], quarter(key[2])
            elif key[0] == "over":
                mx, cols = over_mx[key[1]], quarter(key[2])
            else:
                mx, cols = y_mx, quarter(key[1])
            quantise(mx, cols, staged[key][:])

        def load_matmul(g, q, h):
            bank = psum.tile([P, 2, W], F32, name="bank")
            for e in range(2):
                t = 2 * h + e
                for c in range(J_PASSES):
                    matmul(bank[:, e, :], plan_mx[g, c], slice(t * P, (t + 1) * P), hours_mx[c], quarter(q),
                           c == 0, c == J_PASSES - 1)
            banks["load", g, q, h] = bank

        def subtract(g, q, h):
            if h == 0:
                pairs[g, q] = work.tile([P, 2, W, 2], BF16, name="pairs", bufs=3)
            nc.vector.tensor_tensor(
                out=pairs[g, q][:, h, :, :],
                in0=banks["load", g, q, h][:].rearrange("p e m -> p m e"),
                in1=spare_rows[g, q][:, 2 * h : 2 * h + 2, :].rearrange("p e m -> p m e"),
                op=ALU.subtract,
            )

        def clamp(g, q):
            over = work.tile([P, W * 4], BF16, name="over", bufs=2, align_bytes=64)
            nc.vector.tensor_scalar(
                out=over[:].rearrange("p (m h e) -> p m h e", h=2, e=2),
                in0=pairs[g, q][:].rearrange("p h m e -> p m h e"),
                scalar1=0.0,
                scalar2=None,
                op0=ALU.max,
            )
            staged["over", g, q] = over

        out_rows = out_0.rearrange("(p t) m -> p t m", t=4)
        out_words = out_1[0].rearrange("p m t -> p (m t)").bitcast(I32)
        out_scales = out_2[0].bitcast(I32)

        def cost_matmul(q, h):
            bank = psum.tile([P, 2, W], F32, name="bank")
            for e in range(2):
                for g in range(GROUPS):
                    matmul(bank[:, e, :], rates_mx[2 * h + e], slice(g * P, (g + 1) * P), over_mx[g], quarter(q),
                           g == 0, g == GROUPS - 1)
            banks["cost", q, h] = bank

        def scale_y(q, h):
            if h == 0:
                y_tiles[q] = work.tile([P, 4, W], F32, name="y", bufs=2)
            for e in range(2):
                t = 2 * h + e
                nc.scalar.activation(
                    out=y_tiles[q][:, t, :], in_=banks["cost", q, h][:, e, :], func=ACT.Copy, scale=budget[:, t : t + 1]
                )

        def store_y(q):
            nc.sync.dma_start(out=out_rows[:, :, quarter(q)], in_=y_tiles[q][:])

        def round_y(q):
            y_bf = work.tile([P, W * 4], BF16, name="y_bf", bufs=2, align_bytes=64)
            nc.vector.tensor_copy(
                out=y_bf[:].rearrange("p (m t) -> p m t", t=4), in_=y_tiles[q][:].rearrange("p t m -> p m t")
            )
            staged["y", q] = y_bf

        def store_words(q):
            nc.sync.dma_start(out=out_words[:, quarter(q)], in_=y_mx[0][:, quarter(q)].bitcast(I32))

        def store_scales(q0, q1):
            cols = slice(q0 * W // 4, q1 * W // 4)
            for quad in range(4):
                queue = nc.sync if quad % 2 == 0 else nc.scalar
                queue.dma_start(
                    out=out_scales[4 * quad : 4 * quad + 4, cols],
                    in_=y_mx[1][32 * quad : 32 * quad + 4, :].bitcast(I32)[:, cols],
                )

        run = {"turn": turn, "leave": leave, "weave": weave, "pack": pack, "load": load_matmul, "sub": subtract,
               "clamp": clamp, "cost": cost_matmul, "scale": scale_y, "store_y": store_y, "round": round_y,
               "store_words": store_words, "store_scales": store_scales}
        for step in program():
            run[step[0]](*step[1:])
